import numpy as np
import ml_dtypes


def mxq(x, axis, fmt="e4m3"):
    dtype, down = {"e4m3": (ml_dtypes.float8_e4m3fn, 7), "e5m2": (ml_dtypes.float8_e5m2, 14)}[fmt]
    v = np.moveaxis(np.asarray(x, np.float32).astype(ml_dtypes.bfloat16).astype(np.float64), axis, -1)
    blocks = v.reshape(v.shape[:-1] + (-1, 32))
    amax = np.abs(blocks).max(-1, keepdims=True)
    byte = np.maximum(np.where(amax > 0, np.frexp(amax)[1] - 1 + 127, 0) - down, 1)
    scale = np.exp2(byte - 127.0)
    codes = (blocks / scale).astype(np.float32).astype(dtype).astype(np.float64)
    return np.moveaxis((codes * scale).reshape(v.shape), -1, axis)


WIDE = False


def mx_kscale(k):
    if not WIDE:
        return np.ones(k)
    levels = np.array([10, -10, 5, -5, 0])
    if k % 512:
        return np.exp2(np.random.permutation(np.resize(levels, k // 32))).repeat(32)
    a = np.empty((k // 512, 16))
    for p in range(k // 512):
        a[p, :8] = np.random.permutation(np.resize(levels, 8))
        for g in range(8):
            far = levels[np.abs(levels - a[p, g]) >= 10]
            a[p, g + 8] = far[np.random.randint(len(far))]
    return np.exp2(a.ravel()).repeat(32)


def f64(x):
    return np.asarray(x).astype(np.float64)


def striped(idx):
    return np.tile(idx.reshape(-1, 16).T, (8, 1)).astype(np.uint16)


def unstriped(offs):
    return offs[:16].T.reshape(-1).astype(np.int64)


def pack_weight(w):
    k, n = w.shape
    w = f64(np.asarray(w, np.float32).astype(ml_dtypes.bfloat16)).reshape(k // 32, 32, n)
    amax = np.abs(w).max(1)
    byte = np.clip(np.where(amax > 0, np.frexp(amax)[1] - 1 + 127 - 7, 1), 1, 254)
    scaled = (w * np.exp2(127.0 - byte)[:, None, :]).reshape(k, n).astype(np.float32)
    words = np.ascontiguousarray(scaled.reshape(k // 512, 128, 4, n).transpose(0, 1, 3, 2)).astype(ml_dtypes.float8_e4m3fn).view(np.uint8)
    return words, np.ascontiguousarray(byte.astype(np.uint8).reshape(k // 512, 16, n))


def unpack_weight(words, scales):
    g, p, n, _ = words.shape
    vals = np.ascontiguousarray(words).view(ml_dtypes.float8_e4m3fn).astype(np.float64) * np.repeat(np.exp2(scales.astype(np.float64) - 127.0), 8, axis=1)[..., None]
    return vals.transpose(0, 1, 3, 2).reshape(g * 512, n)


K, T, S, V, D, R, G, W = 1024, 1024, 512, 512, 4, 256, 128, 1024


def setup_inputs():
    n = np.random.standard_normal
    s = mx_kscale(K)[:, None]
    packed_xT = pack_weight(n((K, T)) * s)
    packed_eT = pack_weight(n((K, W)) * s)
    return {
        "x_words": packed_xT[0],
        "x_scales": packed_xT[1],
        "hT": (n((K, V)) / np.sqrt(K) / s).astype(np.float32),
        "e_words": packed_eT[0],
        "e_scales": packed_eT[1],
        "offs": striped(np.random.permutation(T)[:S]),
        "head": striped(np.random.permutation(W)[:R]),
        "cl": striped(np.random.permutation(R)[:G]),
    }


def reference(x_words, x_scales, hT, e_words, e_scales, offs, head, cl):
    hTq = mxq(f64(hT), 0, "e4m3")
    e_head = unpack_weight(e_words, e_scales)[:, unstriped(head)]
    z = hTq.T @ e_head
    ex = np.exp(z - z.max(axis=1, keepdims=True))
    ph = ex / ex.sum(axis=1, keepdims=True)
    xq = unpack_weight(x_words, x_scales)[:, unstriped(offs)]
    y = hTq.T @ xq
    top = y.reshape(len(y), -1, D).max(axis=2)
    ee = np.exp(y - np.repeat(top, D, axis=1))
    total = ee.reshape(len(ee), -1, D).sum(axis=2)
    p = ee / np.repeat(total, D, axis=1)
    return (np.repeat(ph[:, unstriped(cl)], D, axis=1)) * p

from contextlib import ExitStack

import concourse.mybir as mybir

F32 = mybir.dt.float32
BF16 = mybir.dt.bfloat16
I32 = mybir.dt.int32
U32 = mybir.dt.uint32
U16 = mybir.dt.uint16
U8 = mybir.dt.uint8
FP8X4 = mybir.dt.float8_e4m3fn_x4
ALU = mybir.AluOpType
ACT = mybir.ActivationFunctionType
AXIS = mybir.AxisListType

P = 128
PACK = 4
PASSES = 2
K_PASS = P * PACK
STORE = 1024
WORDS = 512
CLUSTERS = 256
GROUP = 4
GROUPS = WORDS // GROUP
POSITIONS = 512
TILES = POSITIONS // P

FLOPS = 2 * PASSES * K_PASS * POSITIONS * (WORDS + CLUSTERS)


def tile_picked_yadap_two_p_kernel(
    tc, x_words, x_scales, hT, e_words, e_scales, offs, head, cl, out
):
    nc = tc.nc
    with ExitStack() as ctx:
        held = ctx.enter_context(tc.tile_pool(name="held", bufs=1))
        psum = ctx.enter_context(tc.psum_pool(name="psum", bufs=1))

        def load_list(name, src):
            t = held.tile([P, src.shape[1]], U16, name=name)
            nc.sync.dma_start(t[:], src)
            return t

        def load_words(name, words, o, queue=nc.sync):
            t = held.tile([P, STORE], I32, name=name)
            queue.dma_start(out=t[:], in_=words[o].rearrange("p n r -> p (n r)").bitcast(I32))
            return t

        def load_scales(name, scales, clearer, queue):
            t = held.tile([P, STORE], U8, name=name)
            clearer.memset(t[:].bitcast(I32), 0)
            for q in range(4):
                queue.dma_start(
                    out=t[32 * q : 32 * q + 4 * PASSES, :].bitcast(I32),
                    in_=scales[:, 4 * q : 4 * q + 4, :].bitcast(I32),
                )
            return t

        def load_h(i, o):
            t = held.tile([P, PACK, P], F32, name="h_raw%d_%d" % (i, o), tag="h_raw%d_%d" % (i, o))
            rows = hT[o * K_PASS : (o + 1) * K_PASS, i * P : (i + 1) * P]
            nc.sync.dma_start(out=t[:], in_=rows.rearrange("(p j) t -> p j t", j=PACK))
            return t

        def gather(name, window, offsets, dtype, tag=None):
            n = 16 * offsets.shape[1]
            t = held.tile([P, n], dtype, name=name, tag=tag or name, align_bytes=64)
            nc.vector.tensor_copy(t[:], window.indirect(offsets[:]))
            return t

        offs_t = load_list("offs_t", offs)
        head_t = load_list("head_t", head)
        xw = [load_words("xw0", x_words, 0, nc.scalar)]
        xs = load_scales("xs", x_scales, nc.vector, nc.sync)
        xw.append(load_words("xw1", x_words, 1))
        h_raw = [[load_h(0, o) for o in range(PASSES)]]
        es = load_scales("es", e_scales, nc.gpsimd, nc.gpsimd)
        h_raw.append([load_h(1, o) for o in range(PASSES)])
        ew = [load_words("ew0", e_words, 0)]
        for i in range(2, TILES):
            h_raw.append([load_h(i, o) for o in range(PASSES)])
        ew.append(load_words("ew1", e_words, 1))
        cl_t = load_list("cl_t", cl)

        def interleave(i):
            grouped = held.tile([P, PASSES, P * PACK], BF16, name="h_bf%d" % i, tag="h_bf%d" % i, align_bytes=64)
            for o in range(PASSES):
                nc.scalar.activation(
                    out=grouped[:, o, :].rearrange("p (c i j) -> p c j i", i=4, j=PACK),
                    in_=h_raw[i][o][:].rearrange("p j (c i) -> p c j i", i=4),
                    func=ACT.Copy,
                )
            return grouped

        def quantize(i, grouped):
            codes = held.tile([P, PASSES * P], U32, name="h_codes%d" % i, align_bytes=64)
            scales = held.tile([P, PASSES * P], U8, name="h_scales%d" % i, align_bytes=64)
            nc.vector.quantize_mx(
                out=codes[:].bitcast(FP8X4),
                scales=scales[:],
                in_=grouped[:].rearrange("p o c -> p (o c)"),
            )
            return codes, scales

        def product(acc, hq, codes, scales):
            for o in range(PASSES):
                nc.tensor.matmul_mx(
                    out=acc,
                    lhsT=hq[0][:, o * P : (o + 1) * P].bitcast(FP8X4),
                    lhsT_scale=hq[1][:, o * P : (o + 1) * P],
                    rhs=codes[o][:].bitcast(FP8X4),
                    rhs_scale=scales[4 * o :, :],
                    start=(o == 0),
                    stop=(o == PASSES - 1),
                )

        def by_group(ap):
            return ap.rearrange("p (v d) -> p v d", d=GROUP)

        def spread(ap):
            return ap.unsqueeze(2).to_broadcast([P, GROUPS, GROUP])

        ee = [None] * TILES
        ph = [None] * TILES
        total = held.tile([P, TILES, GROUPS], F32, name="total")
        zsum = held.tile([P, TILES], F32, name="zsum")
        zinv = held.tile([P, TILES], F32, name="zinv")
        zneg = held.tile([P, TILES], F32, name="zneg")

        y = [None] * TILES
        top = [None] * TILES
        diff = [None] * TILES
        ex = [None] * TILES
        z = [None] * 2

        def word_scores(i):
            y[i] = psum.tile([P, WORDS], F32, name="y%d" % i)
            product(y[i][:], hq[i], xg, xsg)

        def word_top(i):
            top[i] = held.tile([P, GROUPS], F32, name="top%d" % i, tag="h_raw1_1" if i == 0 else "top%d" % i)
            nc.vector.tensor_reduce(out=top[i][:], in_=by_group(y[i][:]), axis=AXIS.X, op=ALU.max)

        def word_exp(i):
            diff[i] = held.tile([P, WORDS], F32, name="diff%d" % i)
            nc.vector.tensor_tensor(out=by_group(diff[i][:]), in0=by_group(y[i][:]), in1=spread(top[i][:]), op=ALU.subtract)
            ee[i] = held.tile([P, WORDS], F32, name="ee%d" % i, tag="h_raw%d_%d" % (3 - i // 2, 1 - i % 2))
            nc.scalar.activation(out=ee[i][:], in_=diff[i][:], func=ACT.Exp)
            pairs = held.tile([P, GROUPS, 2], F32, name="pairs%d" % i)
            nc.gpsimd.tensor_tensor(out=pairs[:], in0=by_group(ee[i][:])[:, :, 0:2], in1=by_group(ee[i][:])[:, :, 2:4], op=ALU.add)
            nc.gpsimd.tensor_tensor(out=total[:, i, :], in0=pairs[:, :, 0], in1=pairs[:, :, 1], op=ALU.add)

        def head_scores(half):
            z[half] = psum.tile([P, 2, CLUSTERS], F32, name="z%d" % half)
            for u in range(2):
                product(z[half][:, u, :], hq[2 * half + u], eg, esg)

        def head_exp(half):
            two = slice(2 * half, 2 * half + 2)
            nc.vector.tensor_reduce(out=zneg[:, two], in_=z[half][:], axis=AXIS.X, op=ALU.max, negate=True)
            for u in range(2):
                i = 2 * half + u
                ex[i] = held.tile([P, CLUSTERS], F32, name="ex%d" % i)
                nc.scalar.activation(
                    out=ex[i][:], in_=z[half][:, u, :], func=ACT.Exp, bias=zneg[:, i : i + 1], accum_out=zsum[:, i : i + 1]
                )

        grouped = [interleave(0)]
        xg = [gather("xg0", xw[0][:].bitcast(U32), offs_t, U32)]
        xsg = gather("xsg", xs[:], offs_t, U8)
        xg.append(gather("xg1", xw[1][:].bitcast(U32), offs_t, U32))
        hq = [quantize(0, grouped[0])]
        word_scores(0)
        grouped.append(interleave(1))
        hq.append(quantize(1, grouped[1]))
        word_scores(1)
        grouped.append(interleave(2))
        grouped.append(interleave(3))
        eg = [gather("eg0", ew[0][:].bitcast(U32), head_t, U32, "h_bf1")]
        word_top(0)
        hq.append(quantize(2, grouped[2]))
        word_exp(0)
        word_scores(2)
        word_top(1)
        esg = gather("esg", es[:], head_t, U8, "h_bf2")
        word_exp(1)
        hq.append(quantize(3, grouped[3]))
        word_scores(3)
        eg.append(gather("eg1", ew[1][:].bitcast(U32), head_t, U32, "h_bf3"))
        head_scores(0)
        head_scores(1)
        word_top(2)
        word_top(3)
        word_exp(2)
        head_exp(0)
        head_exp(1)
        word_exp(3)

        phg = held.tile([P, TILES, GROUPS], F32, name="phg")
        for half in range(2):
            two = slice(2 * half, 2 * half + 2)
            nc.vector.reciprocal(out=zinv[:, two], in_=zsum[:, two])
            for i in range(2 * half, 2 * half + 2):
                ph[i] = held.tile([P, CLUSTERS], F32, name="ph%d" % i)
                nc.vector.tensor_scalar(out=ph[i][:], in0=ex[i][:], scalar1=zinv[:, i : i + 1], scalar2=None, op0=ALU.mult)
            for i in range(2 * half, 2 * half + 2):
                nc.vector.tensor_copy(phg[:, i, :], ph[i][:].indirect(cl_t[:]))

        root = diff[TILES - 1][:].rearrange("p (i v) -> p i v", i=TILES)
        inv = held.tile([P, TILES, GROUPS], F32, name="inv")
        w = held.tile([P, TILES, GROUPS], F32, name="w")
        runs = (slice(0, 1), slice(1, 2), slice(2, 4))
        for run in runs:
            nc.scalar.activation(out=root[:, run, :], in_=total[:, run, :], func=ACT.Abs_reciprocal_sqrt)
            nc.scalar.activation(out=inv[:, run, :], in_=root[:, run, :], func=ACT.Square)
        for run in runs:
            nc.vector.tensor_tensor(out=w[:, run, :], in0=phg[:, run, :], in1=inv[:, run, :], op=ALU.mult)
            for i in range(run.start, run.stop):
                res = held.tile([P, WORDS], F32, name="res%d" % i)
                nc.vector.tensor_tensor(out=by_group(res[:]), in0=by_group(ee[i][:]), in1=spread(w[:, i, :]), op=ALU.mult)
                nc.sync.dma_start(out=out[i * P : (i + 1) * P, :], in_=res[:])
